import numpy as np, ml_dtypes
CORES = [36,164,52,180,100,228,116,244]
N = 8
R, T, B = 8192, 2048, 256
def entries(a): return a.T.reshape(-1)
def pack(v, P): return np.ascontiguousarray(np.asarray(v, np.int32).reshape(-1, P).T)
def lists(rng, how):
    I = rng.integers(0, N * R, (N, T)); E = np.sort(rng.integers(0, T + 1, (N, B)), axis=1)
    if how == "void":
        E = np.zeros((N, B), np.int64)
        for r in range(N): k = np.sort(1 + rng.permutation(B - 2)[:6]); c = np.sort(1 + rng.permutation(T)[:6]); E[r] = np.concatenate([[0], c])[np.searchsorted(k, np.arange(B), side="right")]
        E[rng.integers(N)] = 0
    if how == "one":
        p = rng.permutation(N); z = rng.integers(0, B, N); z[p[0]] = 0; z[p[1]] = B - 1; E = np.where(np.arange(B)[None, :] < z[:, None], 0, T)
        I[p[::2]] = R * p[1] + I[p[::2]] % R
    if how == "single": E = np.broadcast_to(1 + np.arange(B), (N, B)).copy()
    if how == "hotrank": I = R * int(rng.integers(N)) + rng.integers(0, R, (N, T))
    if how == "edge": I = R * rng.integers(0, N, (N, T)) + np.where(rng.random((N, T)) < 0.5, 0, R - 1); E[:, -1] = T
    return {"idx": np.stack([pack(i, 16) for i in I]), "end": np.stack([pack(v, 16) for v in E])}
def setup_inputs(rng):
    return dict({"tab": rng.standard_normal((N, 128, R), dtype=np.float32).astype(ml_dtypes.bfloat16)}, **lists(rng, "uniform"))
def setup_inputs_edge(rng):
    d = setup_inputs(rng); d.update(lists(rng, "edge"))
    for k in ("tab",): d[k] = (d[k].astype(np.float32) * 1048576.0).astype(d[k].dtype)
    return d
def setup_inputs_hotrank(rng):
    d = setup_inputs(rng); d.update(lists(rng, "hotrank"))
    for k in ("tab",): d[k] = (d[k].astype(np.float32) * (1 / 1024.0)).astype(d[k].dtype)
    return d
def setup_inputs_one(rng):
    d = setup_inputs(rng); d.update(lists(rng, "one"))
    return d
def setup_inputs_single(rng):
    d = setup_inputs(rng); d.update(lists(rng, "single"))
    return d
def setup_inputs_void(rng):
    d = setup_inputs(rng); d.update(lists(rng, "void"))
    return d
def check_inputs(x):
    bad = []
    if x["idx"].min() < 0 or x["idx"].max() >= N * R: bad.append("idx out of range")
    if x["end"].min() < 0 or x["end"].max() >= T + 1: bad.append("end out of range")
    if any((np.diff(entries(a)) < 0).any() for a in x["end"]): bad.append("end falls")
    t = x["tab"].astype(np.float32)
    if t.min() < -1e30 or t.max() > 1e30: bad.append("tab beyond -1e30 to 1e30")
    return bad
def reference(tab, idx, end):
    A = np.concatenate(list(tab), axis=1)
    y = np.zeros((N, 128, B), tab.dtype)
    for r in range(N):
        G = A[:, entries(idx[r])]; c = np.concatenate([[0], entries(end[r])])
        for b in range(B):
            if c[b + 1] > c[b]: y[r][:, b] = G[:, c[b]:c[b + 1]].max(axis=1)
    return {"y": y}

@@ -1,0 +1,295 @@
+from concourse.bass import DstId, RemoteDMATransfer
+from concourse.mybir import AluOpType, ActivationFunctionType
+
+N, R, LIST, BAGS, SIM = 8, 8192, 2048, 256, 256
+WHO = (0, 0, 0, 0, 1, 1, 2, 2)
+PLACES = 3
+NL = 4
+ORDER = (4, 1, 5, 2, 6, 3, 7)
+BIG = 9.999e29
+PAD = 8
+WIN = R + 2 * PAD
+MW = 2312
+SW = 2056
+LW = 48
+CH = 4
+CW = R // CH
+
+SCRATCH = {
+    "win": ("sbuf", [128, WIN], "bfloat16"),
+    "ii": ("sbuf", [128, 16], "int32"),
+    "en": ("sbuf", [16, 16], "int32"),
+    "pv": ("sbuf", [16, 16], "int32"),
+    "dd": ("sbuf", [16, 16], "float32"),
+    "t1": ("sbuf", [16, 16], "float32"),
+    "t2": ("sbuf", [16, 16], "float32"),
+    "t3": ("sbuf", [16, 16], "float32"),
+    "ones": ("sbuf", [128, 1024], "float32"),
+    "sel": ("sbuf", [128, 1024], "float32"),
+    "sele": ("sbuf", [16, 128], "float32"),
+    "lland": ("sbuf", [128, NL * LW], "float32"),
+    "lp": ("sbuf", [128, NL * 16], "float32"),
+    "offs": ("sbuf", [128, NL * 160], "uint16"),
+    "neg": ("sbuf", [128, BAGS], "bfloat16"),
+    "res": ("sbuf", [128, NL * BAGS], "bfloat16"),
+    "rland": ("sbuf", [128, N * BAGS], "bfloat16"),
+    "acc": ("sbuf", [128, BAGS], "bfloat16"),
+}
+for _k in range(NL):
+    SCRATCH["gat%d" % _k] = ("sbuf", [128, LIST], "bfloat16")
+    SCRATCH["msk%d" % _k] = ("sbuf", [128, MW], "bfloat16")
+    SCRATCH["scn%d" % _k] = ("sbuf", [128, SW], "bfloat16")
+    SCRATCH["ps%d" % _k] = ("psum", [128, 512], "float32")
+SEMAPHORES = ["pz", "on", "ls", "wf", "ng", "zs", "ldx", "dio", "sel_", "sele_", "e1", "e2", "snd", "loc", "go", "ac", "st"]
+for _k in range(NL):
+    SEMAPHORES += [_n + "%d" % _k for _n in ("mk", "lp_", "pe", "of", "sc", "vg", "sg", "sn", "fi")]
+for _k in range(CH):
+    SEMAPHORES += ["ld%d" % _k, "tc%d" % _k]
+for _k in range(N):
+    SEMAPHORES += ["l%d" % _k, "r%d" % _k]
+
+
+def team(c, topo):
+    near = [d for d in range(SIM) if d != c and topo.host(d) == topo.host(c) and topo.chip(d) == topo.chip(c)
+            and topo.die(d) == topo.die(c)]
+    return ([c] + near)[:PLACES]
+
+
+def bits(m):
+    return bin(m).count("1")
+
+
+def rank_program(g, core, T, topo):
+    me = None
+    for r, c in enumerate(T.cores):
+        if topo.host(c) == topo.host(core) and topo.chip(c) == topo.chip(core):
+            crew = team(c, topo)
+            if core in crew:
+                me = (r, crew.index(core))
+    if me is None:
+        return
+    r, place = me
+    V, S, P, Y = g.vector, g.scalar, g.tensor, g.sync
+    A, F = AluOpType, ActivationFunctionType
+    sem = T.sem
+    js = [j for j in range(N) if WHO[j] == place]
+    nl = len(js)
+    last = nl - 1
+    is_rank = place == 0
+
+    def arrive(k):
+        if js[k] == 0:
+            return sem.snd, 2
+        src = T.cores[(r + js[k]) % N]
+        return sem["l%d" % ((r + js[k]) % N)], bits(topo.mask(src, core))
+
+    def table(q):
+        q.wait_ge(sem.wf, 2)
+        for c in range(CH):
+            if is_rank:
+                q.wait_ge(sem["ld%d" % c], 16)
+            else:
+                q.wait_ge(sem["tc%d" % c], bits(topo.mask(crew[place - 1], core)))
+
+    cut = [1600] * nl
+    cut[last] = 1216
+    if not is_rank:
+        cut = [1216] * nl
+
+    if is_rank:
+        S.dma_start(out=T.en[:, :], in_=T.end[:, :]).then_inc(sem.ldx, 16)
+        S.dma_start(out=T.ii[:, :], in_=T.idx[:, :]).then_inc(sem.ldx, 16)
+        S.wait_ge(sem.pz, 1)
+        S.dma_start(out=T.pv[1:16, :], in_=T.end[0:15, :]).then_inc(sem.ldx, 16)
+        S.dma_start(out=T.pv[0:1, 1:16], in_=T.end[15:16, 0:15]).then_inc(sem.ldx, 16)
+        for c in range(CH):
+            if c == CH // 2:
+                Y.wait_ge(sem.go, 1)
+            Y.dma_start(out=T.win[:, PAD + c * CW:PAD + (c + 1) * CW], in_=T.tab[:, c * CW:(c + 1) * CW]).then_inc(sem["ld%d" % c], 16)
+
+    if is_rank:
+        V.memset(T.pv[:, :], 0).then_inc(sem.pz, 1)
+    V.memset(T.ones[:, :], 1.0).then_inc(sem.on, 1)
+    if is_rank:
+        V.memset(T.lland[:, 16:LW], 0.0).then_inc(sem.ls, 1)
+    V.memset(T.win[:, 0:PAD], -BIG).then_inc(sem.wf, 1)
+    V.memset(T.win[:, PAD + R:WIN], -BIG).then_inc(sem.wf, 1)
+    V.memset(T.neg[:, :], -BIG).then_inc(sem.ng, 1)
+    for k in range(nl):
+        V.memset(T["scn%d" % k][:, 0:2], 0.0).then_inc(sem.zs, 1)
+
+    by_s = (2, 3) if is_rank else ()
+    mk = {}
+
+    def base(k):
+        V.memset(T["msk%d" % k][:, 0:1], -BIG).then_inc(sem["mk%d" % k], 1)
+        if k in by_s:
+            V.memset(T["msk%d" % k][:, 1:8], BIG).then_inc(sem["mk%d" % k], 1)
+            V.memset(T["msk%d" % k][:, 2056:MW], BIG).then_inc(sem["mk%d" % k], 1)
+            mk[k] = 5
+        else:
+            V.memset(T["msk%d" % k][:, 1:MW], BIG).then_inc(sem["mk%d" % k], 1)
+            mk[k] = 2
+
+    base(0)
+    if is_rank:
+        V.wait_ge(sem.ldx, 64)
+        V.wait_ge(sem.ls, 1)
+        V.wait_ge(sem.dio, 1)
+        V.tensor_tensor(T.t1[:, :], T.en[:, :], T.pv[:, :], A.is_gt).then_inc(sem.e1, 1)
+        V.tensor_tensor(T.t2[:, :], T.en[:, :], T.pv[:, :], A.is_le).then_inc(sem.e1, 1)
+        V.tensor_copy(T.lland[:, 0:16], T.ii[:, :]).then_inc(sem.snd, 1)
+        V.wait_ge(sem.e1, 2)
+        V.tensor_tensor(T.lland[0:16, 32:48], T.en[:, :], T.t1[:, :], A.mult).then_inc(sem.e2, 1)
+        V.tensor_tensor(T.t3[:, :], T.dd[:, :], T.t2[:, :], A.mult).then_inc(sem.e2, 1)
+        V.wait_ge(sem.e2, 2)
+        V.tensor_tensor(T.lland[0:16, 16:32], T.lland[0:16, 32:48], T.t3[:, :], A.add).then_inc(sem.snd, 1)
+
+    def prep(k):
+        s_, n_ = arrive(k)
+        V.wait_ge(s_, n_)
+        V.tensor_scalar(T.lp[:, k * 16:(k + 1) * 16], T.lland[:, k * LW:k * LW + 16], float(PAD - R * r), float(PAD + R),
+                        op0=A.add, op1=A.min).then_inc(sem["lp_%d" % k], 1)
+
+    def offsets(k):
+        V.wait_ge(sem["pe%d" % k], 9)
+        V.tensor_copy(T.offs[:, k * 160:(k + 1) * 160], T["ps%d" % k][:, 0:160]).then_inc(sem["of%d" % k], 1)
+
+    def marks(k):
+        V.wait_ge(sem["of%d" % k], 1)
+        V.wait_ge(sem.ng, 1)
+        V.wait_ge(sem["mk%d" % k], mk[k])
+        V.tensor_copy(T["msk%d" % k][:, :].indirect(T.offs[:, k * 160 + 128:k * 160 + 144]), T.neg[:, :]).then_inc(sem["sc%d" % k], 1)
+
+    def gather_v(k):
+        V.wait_ge(sem["of%d" % k], 1)
+        V.tensor_copy(T["gat%d" % k][:, cut[k]:LIST],
+                      T.win[:, :].indirect(T.offs[:, k * 160 + cut[k] // 16:k * 160 + 128])).then_inc(sem["vg%d" % k], 1)
+
+    def scan(k):
+        V.wait_ge(sem["sc%d" % k], 1)
+        V.wait_ge(sem["vg%d" % k], 1)
+        V.wait_ge(sem["sg%d" % k], 1)
+        V.tensor_tensor_scan(T["scn%d" % k][:, 2:2 + LIST], T["msk%d" % k][:, 0:LIST], T["gat%d" % k][:, :], 0.0,
+                             A.min, A.max).then_inc(sem["sn%d" % k], 1)
+
+    prep(0)
+    if is_rank:
+        for k in range(1, nl):
+            base(k)
+            if k == 1:
+                offsets(0)
+                marks(0)
+        for k in range(nl):
+            if k < last:
+                prep(k + 1)
+            if k == 0:
+                table(V)
+            gather_v(k)
+            if k < last:
+                offsets(k + 1)
+                marks(k + 1)
+            scan(k)
+    else:
+        for k in range(1, nl):
+            base(k)
+        for k in range(1, nl):
+            prep(k)
+        for k in range(nl):
+            offsets(k)
+            marks(k)
+        table(V)
+        for k in range(nl):
+            gather_v(k)
+            scan(k)
+    if is_rank:
+        V.wait_ge(sem.fi0, 1)
+        for n_, j in enumerate(ORDER):
+            frm = team(T.cores[(r - j) % N], topo)[WHO[j]]
+            V.wait_ge(sem["r%d" % j], bits(topo.mask(frm, core)))
+            if n_:
+                V.wait_ge(sem.ac, n_)
+            V.tensor_tensor(T.acc[:, :], T.acc[:, :] if n_ else T.rland[:, 0:BAGS], T.rland[:, j * BAGS:(j + 1) * BAGS],
+                            A.max).then_inc(sem.ac, 1)
+        Y.wait_ge(sem.ac, len(ORDER))
+        Y.dma_start(out=T.y[:, :], in_=T.acc[:, :]).then_inc(sem.st, 16)
+        Y.wait_ge(sem.st, 16)
+
+    P.wait_ge(sem.sel_, 1)
+    P.wait_ge(sem.sele_, 1)
+    for k in range(nl):
+        P.wait_ge(*arrive(k))
+        P.wait_ge(sem["lp_%d" % k], 1)
+        ps = T["ps%d" % k]
+        for h in range(8):
+            P.matmul(ps[:, h * 16:(h + 1) * 16], T.sel[:, h * 128:(h + 1) * 128], T.lp[:, k * 16:(k + 1) * 16],
+                     True, True).then_inc(sem["pe%d" % k], 1)
+        P.matmul(ps[:, 128:160], T.sele[:, :], T.lland[0:16, k * LW + 16:(k + 1) * LW], True, True).then_inc(sem["pe%d" % k], 1)
+
+    if by_s:
+        S.wait_ge(sem.on, 1)
+    for k in by_s:
+        for a in (8, 1032):
+            S.activation(T["msk%d" % k][:, a:a + 1024], T.ones[:, :], F.Identity, bias=BIG, scale=0.0).then_inc(sem["mk%d" % k], 1)
+
+    def fetch(k):
+        S.wait_ge(sem["sn%d" % k], 1)
+        S.wait_ge(sem.zs, nl)
+        out = T.rland[:, 0:BAGS] if js[k] == 0 else T.res[:, k * BAGS:(k + 1) * BAGS]
+        S.activation(out, T["scn%d" % k][:, 1:2 + LIST].indirect(T.offs[:, k * 160 + 144:k * 160 + 160]), F.Copy).then_inc(sem["fi%d" % k], 1)
+
+    for k in range(nl):
+        S.wait_ge(sem["of%d" % k], 1)
+        if k == 0:
+            table(S)
+        S.activation(T["gat%d" % k][:, 0:cut[k]], T.win[:, :].indirect(T.offs[:, k * 160:k * 160 + cut[k] // 16]),
+                     F.Copy).then_inc(sem["sg%d" % k], 1)
+        if k:
+            fetch(k - 1)
+    fetch(last)
+
+    sent = 0
+    if is_rank:
+        g.iota(T.dd[:, :], [[16, 16]], LIST + 1, 1, allow_small_or_imprecise_dtypes=True).then_inc(sem.dio, 1)
+    g.wait_ge(sem.on, 1)
+    g.affine_select(T.sele[:, :], T.ones[0:16, 0:128], [[0, 8], [-1, 16]], A.is_equal, 0.0, 0, 1).then_inc(sem.sele_, 1)
+    g.affine_select(T.sel[:, :], T.ones[:, :], [[-1, 8], [0, 8], [-8, 16]], A.is_equal, 0.0, 0, 1).then_inc(sem.sel_, 1)
+    if is_rank:
+        ids, dsts, m = [], [], None
+        for j in range(1, N):
+            d = team(T.cores[(r - j) % N], topo)[WHO[j]]
+            slot = [q for q in range(N) if WHO[q] == WHO[j]].index(j)
+            rid, pid = topo.addr(d, core)
+            ids.append(DstId(rid=rid, pnc=pid))
+            dsts.append(T.lland[:, slot * LW:(slot + 1) * LW])
+            m = topo.mask(core, d)
+        g.wait_ge(sem.snd, 2)
+        g.wait_ge(sem.ls, 1)
+        g.wait_ge(sem.e2, 2)
+        g.remote_dma_fused([RemoteDMATransfer(dst_ids=ids, dma_engine_mask=m, remote_sem=sem["l%d" % r],
+                                              srcs=[T.lland[:, 0:LW]], dsts=dsts)], local_sem=sem.loc)
+        sent += bits(m)
+        g.sem_inc(sem.go, 1)
+    if place + 1 < PLACES:
+        d = crew[place + 1]
+        m = topo.mask(core, d)
+        rid, pid = topo.addr(d, core)
+        for c in range(CH):
+            if is_rank:
+                g.wait_ge(sem["ld%d" % c], 16)
+            else:
+                g.wait_ge(sem["tc%d" % c], bits(topo.mask(crew[place - 1], core)))
+            w = T.win[:, PAD + c * CW:PAD + (c + 1) * CW]
+            g.remote_dma(w, w, sem["tc%d" % c], sem.loc, pid, rid, m)
+            sent += bits(m)
+    for k in range(nl):
+        if js[k] == 0:
+            continue
+        d = T.cores[(r + js[k]) % N]
+        m = topo.mask(core, d)
+        rid, pid = topo.addr(d, core)
+        g.wait_ge(sem["fi%d" % k], 1)
+        g.remote_dma(T.rland[:, js[k] * BAGS:(js[k] + 1) * BAGS], T.res[:, k * BAGS:(k + 1) * BAGS], sem["r%d" % js[k]], sem.loc,
+                     pid, rid, m)
+        sent += bits(m)
+    g.wait_ge(sem.loc, sent)

@@ -2,47 +2,53 @@ from concourse.bass import DstId, RemoteDMATransfer
 from concourse.mybir import AluOpType, ActivationFunctionType
 
 N, R, LIST, BAGS, SIM = 8, 8192, 2048, 256, 256
-WHO = (0, 0, 0, 0, 1, 1, 2, 2)
-PLACES = 3
-NL = 4
-ORDER = (4, 1, 5, 2, 6, 3, 7)
+WHO = (0, 0, 0, 1, 1, 2, 2, 2)
+ORDER = (5, 3, 1, 6, 2, 4, 7)
+SEND = (1, 2, 5, 3, 6, 4, 7)
+CUT = (1600, 1408, 1216)
+PLACES = max(WHO) + 1
+NL = max([WHO.count(_k) for _k in range(PLACES)])
 BIG = 9.999e29
 PAD = 8
 WIN = R + 2 * PAD
 MW = 2312
 SW = 2056
-LW = 48
-CH = 4
-CW = R // CH
+LW = 160
+SIZES = (2048, 2048, 2048, 2048)
+HOME = (1, 2, 1, 2)
+EARLY = 3
+FIRST = 1
+CH = len(SIZES)
 
 SCRATCH = {
     "win": ("sbuf", [128, WIN], "bfloat16"),
-    "ii": ("sbuf", [128, 16], "int32"),
+    "ii": ("sbuf", [16, 128], "int32"),
     "en": ("sbuf", [16, 16], "int32"),
     "pv": ("sbuf", [16, 16], "int32"),
     "dd": ("sbuf", [16, 16], "float32"),
     "t1": ("sbuf", [16, 16], "float32"),
     "t2": ("sbuf", [16, 16], "float32"),
     "t3": ("sbuf", [16, 16], "float32"),
-    "ones": ("sbuf", [128, 1024], "float32"),
-    "sel": ("sbuf", [128, 1024], "float32"),
+    "ie": ("sbuf", [16, 128], "float32"),
     "sele": ("sbuf", [16, 128], "float32"),
-    "lland": ("sbuf", [128, NL * LW], "float32"),
-    "lp": ("sbuf", [128, NL * 16], "float32"),
+    "wl": ("sbuf", [16, NL * LW], "float32"),
+    "wsend": ("dram", [128, 20], "float32"),
+    "wland": ("dram", [NL, 128, 20], "float32"),
     "offs": ("sbuf", [128, NL * 160], "uint16"),
-    "neg": ("sbuf", [128, BAGS], "bfloat16"),
+    "neg": ("sbuf", [128, 1024], "bfloat16"),
     "res": ("sbuf", [128, NL * BAGS], "bfloat16"),
     "rland": ("sbuf", [128, N * BAGS], "bfloat16"),
     "acc": ("sbuf", [128, BAGS], "bfloat16"),
+    "pacc": ("psum", [128, 512], "float32"),
 }
 for _k in range(NL):
     SCRATCH["gat%d" % _k] = ("sbuf", [128, LIST], "bfloat16")
     SCRATCH["msk%d" % _k] = ("sbuf", [128, MW], "bfloat16")
     SCRATCH["scn%d" % _k] = ("sbuf", [128, SW], "bfloat16")
     SCRATCH["ps%d" % _k] = ("psum", [128, 512], "float32")
-SEMAPHORES = ["pz", "on", "ls", "wf", "ng", "zs", "ldx", "dio", "sel_", "sele_", "e1", "e2", "snd", "loc", "go", "ac", "st"]
+SEMAPHORES = ["pz", "on", "wf", "ng", "zs", "ldx", "dio", "sele_", "e1", "e2", "snd", "sto", "loc", "ac", "st"]
 for _k in range(NL):
-    SEMAPHORES += [_n + "%d" % _k for _n in ("mk", "lp_", "pe", "of", "sc", "vg", "sg", "sn", "fi")]
+    SEMAPHORES += [_n + "%d" % _k for _n in ("mk", "pe", "wl", "of", "sc", "vg", "sg", "sn", "fi")]
 for _k in range(CH):
     SEMAPHORES += ["ld%d" % _k, "tc%d" % _k]
 for _k in range(N):
@@ -77,48 +83,63 @@ def rank_program(g, core, T, topo):
     last = nl - 1
     is_rank = place == 0
 
-    def arrive(k):
-        if js[k] == 0:
-            return sem.snd, 2
-        src = T.cores[(r + js[k]) % N]
-        return sem["l%d" % ((r + js[k]) % N)], bits(topo.mask(src, core))
+    def chunk(c):
+        a = PAD + sum(SIZES[:c])
+        return T.win[:, a:a + SIZES[c]]
+
+    def came(c):
+        return bits(topo.mask(crew[0 if HOME[c] == place else HOME[c]], core))
 
     def table(q):
         q.wait_ge(sem.wf, 2)
         for c in range(CH):
-            if is_rank:
-                q.wait_ge(sem["ld%d" % c], 16)
-            else:
-                q.wait_ge(sem["tc%d" % c], bits(topo.mask(crew[place - 1], core)))
+            q.wait_ge(sem["ld%d" % c] if is_rank else sem["tc%d" % c], 16 if is_rank else came(c))
 
-    cut = [1600] * nl
-    cut[last] = 1216
-    if not is_rank:
-        cut = [1216] * nl
+    cut = [CUT[0] if is_rank else CUT[2]] * nl
+    if is_rank:
+        cut[last] = CUT[1]
 
     if is_rank:
-        S.dma_start(out=T.en[:, :], in_=T.end[:, :]).then_inc(sem.ldx, 16)
         S.dma_start(out=T.ii[:, :], in_=T.idx[:, :]).then_inc(sem.ldx, 16)
+        Y.dma_start(out=T.en[:, :], in_=T.end[:, :]).then_inc(sem.ldx, 16)
         S.wait_ge(sem.pz, 1)
-        S.dma_start(out=T.pv[1:16, :], in_=T.end[0:15, :]).then_inc(sem.ldx, 16)
         S.dma_start(out=T.pv[0:1, 1:16], in_=T.end[15:16, 0:15]).then_inc(sem.ldx, 16)
+        Y.wait_ge(sem.pz, 1)
+        Y.dma_start(out=T.pv[1:16, :], in_=T.end[0:15, :]).then_inc(sem.ldx, 16)
         for c in range(CH):
-            if c == CH // 2:
-                Y.wait_ge(sem.go, 1)
-            Y.dma_start(out=T.win[:, PAD + c * CW:PAD + (c + 1) * CW], in_=T.tab[:, c * CW:(c + 1) * CW]).then_inc(sem["ld%d" % c], 16)
+            if c == EARLY:
+                Y.wait_ge(sem.snd, 2)
+                Y.wait_ge(sem.e2, 2)
+                Y.dma_start(out=T.wsend[:, :], in_=T.wl[:, 0:LW]).then_inc(sem.sto, 16)
+            a = sum(SIZES[:c])
+            Y.dma_start(out=chunk(c), in_=T.tab[:, a:a + SIZES[c]]).then_inc(sem["ld%d" % c], 16)
+    for k in range(nl):
+        if js[k]:
+            src = (r + js[k]) % N
+            Y.wait_ge(sem["l%d" % src], bits(topo.mask(T.cores[src], core)))
+            Y.dma_start(out=T.wl[:, k * LW:(k + 1) * LW], in_=T.wland[k]).then_inc(sem["wl%d" % k], 16)
 
     if is_rank:
         V.memset(T.pv[:, :], 0).then_inc(sem.pz, 1)
-    V.memset(T.ones[:, :], 1.0).then_inc(sem.on, 1)
-    if is_rank:
-        V.memset(T.lland[:, 16:LW], 0.0).then_inc(sem.ls, 1)
+    V.memset(T.neg[:, :], -BIG).then_inc(sem.ng, 1)
+    V.wait_ge(sem.on, 1)
+    V.tensor_scalar(T.sele[:, :], T.ie[:, :], 0.0, None, op0=A.is_equal).then_inc(sem.sele_, 1)
     V.memset(T.win[:, 0:PAD], -BIG).then_inc(sem.wf, 1)
     V.memset(T.win[:, PAD + R:WIN], -BIG).then_inc(sem.wf, 1)
-    V.memset(T.neg[:, :], -BIG).then_inc(sem.ng, 1)
-    for k in range(nl):
-        V.memset(T["scn%d" % k][:, 0:2], 0.0).then_inc(sem.zs, 1)
 
-    by_s = (2, 3) if is_rank else ()
+    if is_rank:
+        V.wait_ge(sem.ldx, 64)
+        V.wait_ge(sem.dio, 1)
+        V.tensor_tensor(T.t1[:, :], T.en[:, :], T.pv[:, :], A.is_gt).then_inc(sem.e1, 1)
+        V.tensor_tensor(T.t2[:, :], T.en[:, :], T.pv[:, :], A.is_le).then_inc(sem.e1, 1)
+        V.tensor_copy(T.wl[:, 0:128], T.ii[:, :]).then_inc(sem.snd, 1)
+        V.wait_ge(sem.e1, 2)
+        V.tensor_tensor(T.wl[:, 144:160], T.en[:, :], T.t1[:, :], A.mult).then_inc(sem.e2, 1)
+        V.tensor_tensor(T.t3[:, :], T.dd[:, :], T.t2[:, :], A.mult).then_inc(sem.e2, 1)
+        V.wait_ge(sem.e2, 2)
+        V.tensor_tensor(T.wl[:, 128:144], T.wl[:, 144:160], T.t3[:, :], A.add).then_inc(sem.snd, 1)
+
+    by_s = range(2, nl) if is_rank else ()
     mk = {}
 
     def base(k):
@@ -131,38 +152,20 @@ def rank_program(g, core, T, topo):
             V.memset(T["msk%d" % k][:, 1:MW], BIG).then_inc(sem["mk%d" % k], 1)
             mk[k] = 2
 
-    base(0)
-    if is_rank:
-        V.wait_ge(sem.ldx, 64)
-        V.wait_ge(sem.ls, 1)
-        V.wait_ge(sem.dio, 1)
-        V.tensor_tensor(T.t1[:, :], T.en[:, :], T.pv[:, :], A.is_gt).then_inc(sem.e1, 1)
-        V.tensor_tensor(T.t2[:, :], T.en[:, :], T.pv[:, :], A.is_le).then_inc(sem.e1, 1)
-        V.tensor_copy(T.lland[:, 0:16], T.ii[:, :]).then_inc(sem.snd, 1)
-        V.wait_ge(sem.e1, 2)
-        V.tensor_tensor(T.lland[0:16, 32:48], T.en[:, :], T.t1[:, :], A.mult).then_inc(sem.e2, 1)
-        V.tensor_tensor(T.t3[:, :], T.dd[:, :], T.t2[:, :], A.mult).then_inc(sem.e2, 1)
-        V.wait_ge(sem.e2, 2)
-        V.tensor_tensor(T.lland[0:16, 16:32], T.lland[0:16, 32:48], T.t3[:, :], A.add).then_inc(sem.snd, 1)
-
-    def prep(k):
-        s_, n_ = arrive(k)
-        V.wait_ge(s_, n_)
-        V.tensor_scalar(T.lp[:, k * 16:(k + 1) * 16], T.lland[:, k * LW:k * LW + 16], float(PAD - R * r), float(PAD + R),
-                        op0=A.add, op1=A.min).then_inc(sem["lp_%d" % k], 1)
-
     def offsets(k):
-        V.wait_ge(sem["pe%d" % k], 9)
-        V.tensor_copy(T.offs[:, k * 160:(k + 1) * 160], T["ps%d" % k][:, 0:160]).then_inc(sem["of%d" % k], 1)
+        V.wait_ge(sem["pe%d" % k], 1)
+        V.tensor_scalar(T.offs[:, k * 160:k * 160 + 128], T["ps%d" % k][:, 0:128], float(PAD - R * r), float(PAD + R),
+                        op0=A.add, op1=A.min).then_inc(sem["of%d" % k], 1)
+        V.tensor_copy(T.offs[:, k * 160 + 128:(k + 1) * 160], T["ps%d" % k][:, 128:160]).then_inc(sem["of%d" % k], 1)
 
     def marks(k):
-        V.wait_ge(sem["of%d" % k], 1)
+        V.wait_ge(sem["of%d" % k], 2)
         V.wait_ge(sem.ng, 1)
         V.wait_ge(sem["mk%d" % k], mk[k])
-        V.tensor_copy(T["msk%d" % k][:, :].indirect(T.offs[:, k * 160 + 128:k * 160 + 144]), T.neg[:, :]).then_inc(sem["sc%d" % k], 1)
+        V.tensor_copy(T["msk%d" % k][:, :].indirect(T.offs[:, k * 160 + 128:k * 160 + 144]), T.neg[:, 0:BAGS]).then_inc(sem["sc%d" % k], 1)
 
     def gather_v(k):
-        V.wait_ge(sem["of%d" % k], 1)
+        V.wait_ge(sem["of%d" % k], 2)
         V.tensor_copy(T["gat%d" % k][:, cut[k]:LIST],
                       T.win[:, :].indirect(T.offs[:, k * 160 + cut[k] // 16:k * 160 + 128])).then_inc(sem["vg%d" % k], 1)
 
@@ -173,35 +176,43 @@ def rank_program(g, core, T, topo):
         V.tensor_tensor_scan(T["scn%d" % k][:, 2:2 + LIST], T["msk%d" % k][:, 0:LIST], T["gat%d" % k][:, :], 0.0,
                              A.min, A.max).then_inc(sem["sn%d" % k], 1)
 
-    prep(0)
+    def target(k):
+        return (T.rland, 0) if js[k] == 0 else (T.res, k * BAGS)
+
+    half = BAGS // 2
     if is_rank:
+        base(0)
+        offsets(0)
+        marks(0)
         for k in range(1, nl):
             base(k)
-            if k == 1:
-                offsets(0)
-                marks(0)
+    else:
         for k in range(nl):
-            if k < last:
-                prep(k + 1)
-            if k == 0:
-                table(V)
+            base(k)
+    for k in range(nl):
+        V.memset(T["scn%d" % k][:, 0:2], 0.0).then_inc(sem.zs, 1)
+    if is_rank:
+        table(V)
+        gather_v(0)
+        scan(0)
+        for k in range(1, nl):
+            offsets(k)
+            marks(k)
             gather_v(k)
-            if k < last:
-                offsets(k + 1)
-                marks(k + 1)
             scan(k)
     else:
-        for k in range(1, nl):
-            base(k)
-        for k in range(1, nl):
-            prep(k)
         for k in range(nl):
             offsets(k)
+        for k in range(nl):
             marks(k)
         table(V)
         for k in range(nl):
             gather_v(k)
             scan(k)
+    V.wait_ge(sem["sn%d" % last], 1)
+    V.wait_ge(sem.zs, nl)
+    buf, a = target(last)
+    V.tensor_copy(buf[:, a + half:a + BAGS], T["scn%d" % last][:, 1:2 + LIST].indirect(T.offs[:, last * 160 + 152:last * 160 + 160])).then_inc(sem["fi%d" % last], 1)
     if is_rank:
         V.wait_ge(sem.fi0, 1)
         for n_, j in enumerate(ORDER):
@@ -209,78 +220,69 @@ def rank_program(g, core, T, topo):
             V.wait_ge(sem["r%d" % j], bits(topo.mask(frm, core)))
             if n_:
                 V.wait_ge(sem.ac, n_)
-            V.tensor_tensor(T.acc[:, :], T.acc[:, :] if n_ else T.rland[:, 0:BAGS], T.rland[:, j * BAGS:(j + 1) * BAGS],
-                            A.max).then_inc(sem.ac, 1)
+            V.tensor_tensor(T.acc[:, :] if n_ == len(ORDER) - 1 else T.pacc[:, 0:BAGS],
+                            T.pacc[:, 0:BAGS] if n_ else T.rland[:, 0:BAGS],
+                            T.rland[:, j * BAGS:(j + 1) * BAGS], A.max).then_inc(sem.ac, 1)
         Y.wait_ge(sem.ac, len(ORDER))
         Y.dma_start(out=T.y[:, :], in_=T.acc[:, :]).then_inc(sem.st, 16)
         Y.wait_ge(sem.st, 16)
 
-    P.wait_ge(sem.sel_, 1)
     P.wait_ge(sem.sele_, 1)
     for k in range(nl):
-        P.wait_ge(*arrive(k))
-        P.wait_ge(sem["lp_%d" % k], 1)
-        ps = T["ps%d" % k]
-        for h in range(8):
-            P.matmul(ps[:, h * 16:(h + 1) * 16], T.sel[:, h * 128:(h + 1) * 128], T.lp[:, k * 16:(k + 1) * 16],
-                     True, True).then_inc(sem["pe%d" % k], 1)
-        P.matmul(ps[:, 128:160], T.sele[:, :], T.lland[0:16, k * LW + 16:(k + 1) * LW], True, True).then_inc(sem["pe%d" % k], 1)
+        if js[k] == 0:
+            P.wait_ge(sem.snd, 2)
+            P.wait_ge(sem.e2, 2)
+        else:
+            P.wait_ge(sem["wl%d" % k], 16)
+        P.matmul(T["ps%d" % k][:, 0:LW], T.sele[:, :], T.wl[:, k * LW:(k + 1) * LW], True, True).then_inc(sem["pe%d" % k], 1)
 
     if by_s:
-        S.wait_ge(sem.on, 1)
+        S.wait_ge(sem.ng, 1)
     for k in by_s:
         for a in (8, 1032):
-            S.activation(T["msk%d" % k][:, a:a + 1024], T.ones[:, :], F.Identity, bias=BIG, scale=0.0).then_inc(sem["mk%d" % k], 1)
+            S.activation(T["msk%d" % k][:, a:a + 1024], T.neg[:, :], F.Copy, scale=-1.0).then_inc(sem["mk%d" % k], 1)
 
-    def fetch(k):
+    def fetch(k, n):
         S.wait_ge(sem["sn%d" % k], 1)
         S.wait_ge(sem.zs, nl)
-        out = T.rland[:, 0:BAGS] if js[k] == 0 else T.res[:, k * BAGS:(k + 1) * BAGS]
-        S.activation(out, T["scn%d" % k][:, 1:2 + LIST].indirect(T.offs[:, k * 160 + 144:k * 160 + 160]), F.Copy).then_inc(sem["fi%d" % k], 1)
+        buf, a = target(k)
+        S.activation(buf[:, a:a + n], T["scn%d" % k][:, 1:2 + LIST].indirect(T.offs[:, k * 160 + 144:k * 160 + 144 + n // 16]), F.Copy).then_inc(sem["fi%d" % k], 1)
 
     for k in range(nl):
-        S.wait_ge(sem["of%d" % k], 1)
+        S.wait_ge(sem["of%d" % k], 2)
         if k == 0:
             table(S)
         S.activation(T["gat%d" % k][:, 0:cut[k]], T.win[:, :].indirect(T.offs[:, k * 160:k * 160 + cut[k] // 16]),
                      F.Copy).then_inc(sem["sg%d" % k], 1)
         if k:
-            fetch(k - 1)
-    fetch(last)
+            fetch(k - 1, BAGS)
+    fetch(last, half)
 
     sent = 0
+    g.iota(T.ie[:, :], [[0, 8], [-1, 16]], 0, 1, allow_small_or_imprecise_dtypes=True).then_inc(sem.on, 1)
     if is_rank:
         g.iota(T.dd[:, :], [[16, 16]], LIST + 1, 1, allow_small_or_imprecise_dtypes=True).then_inc(sem.dio, 1)
-    g.wait_ge(sem.on, 1)
-    g.affine_select(T.sele[:, :], T.ones[0:16, 0:128], [[0, 8], [-1, 16]], A.is_equal, 0.0, 0, 1).then_inc(sem.sele_, 1)
-    g.affine_select(T.sel[:, :], T.ones[:, :], [[-1, 8], [0, 8], [-8, 16]], A.is_equal, 0.0, 0, 1).then_inc(sem.sel_, 1)
-    if is_rank:
-        ids, dsts, m = [], [], None
-        for j in range(1, N):
-            d = team(T.cores[(r - j) % N], topo)[WHO[j]]
-            slot = [q for q in range(N) if WHO[q] == WHO[j]].index(j)
-            rid, pid = topo.addr(d, core)
-            ids.append(DstId(rid=rid, pnc=pid))
-            dsts.append(T.lland[:, slot * LW:(slot + 1) * LW])
-            m = topo.mask(core, d)
-        g.wait_ge(sem.snd, 2)
-        g.wait_ge(sem.ls, 1)
-        g.wait_ge(sem.e2, 2)
-        g.remote_dma_fused([RemoteDMATransfer(dst_ids=ids, dma_engine_mask=m, remote_sem=sem["l%d" % r],
-                                              srcs=[T.lland[:, 0:LW]], dsts=dsts)], local_sem=sem.loc)
-        sent += bits(m)
-        g.sem_inc(sem.go, 1)
-    if place + 1 < PLACES:
-        d = crew[place + 1]
-        m = topo.mask(core, d)
-        rid, pid = topo.addr(d, core)
-        for c in range(CH):
-            if is_rank:
-                g.wait_ge(sem["ld%d" % c], 16)
-            else:
-                g.wait_ge(sem["tc%d" % c], bits(topo.mask(crew[place - 1], core)))
-            w = T.win[:, PAD + c * CW:PAD + (c + 1) * CW]
-            g.remote_dma(w, w, sem["tc%d" % c], sem.loc, pid, rid, m)
+    for c in range(CH):
+        if is_rank and c == FIRST:
+            ids, dsts, m = [], [], None
+            for j in SEND:
+                d = team(T.cores[(r - j) % N], topo)[WHO[j]]
+                slot = [q for q in range(N) if WHO[q] == WHO[j]].index(j)
+                rid, pid = topo.addr(d, core)
+                ids.append(DstId(rid=rid, pnc=pid))
+                dsts.append(T.wland[slot])
+                m = topo.mask(core, d)
+            g.wait_ge(sem.sto, 16)
+            g.remote_dma_fused([RemoteDMATransfer(dst_ids=ids, dma_engine_mask=m, remote_sem=sem["l%d" % r],
+                                                  srcs=[T.wsend[:, :]], dsts=dsts)], local_sem=sem.loc)
+            sent += bits(m)
+        if not is_rank and HOME[c] != place:
+            continue
+        g.wait_ge(sem["ld%d" % c] if is_rank else sem["tc%d" % c], 16 if is_rank else came(c))
+        for p in [HOME[c]] if is_rank else [p for p in range(1, PLACES) if p != place]:
+            m = topo.mask(core, crew[p])
+            rid, pid = topo.addr(crew[p], core)
+            g.remote_dma(chunk(c), chunk(c), sem["tc%d" % c], sem.loc, pid, rid, m)
             sent += bits(m)
     for k in range(nl):
         if js[k] == 0:
@@ -288,7 +290,7 @@ def rank_program(g, core, T, topo):
         d = T.cores[(r + js[k]) % N]
         m = topo.mask(core, d)
         rid, pid = topo.addr(d, core)
-        g.wait_ge(sem["fi%d" % k], 1)
+        g.wait_ge(sem["fi%d" % k], 2 if k == last else 1)
         g.remote_dma(T.rland[:, js[k] * BAGS:(js[k] + 1) * BAGS], T.res[:, k * BAGS:(k + 1) * BAGS], sem["r%d" % js[k]], sem.loc,
                      pid, rid, m)
         sent += bits(m)

from concourse.bass import DstId, RemoteDMATransfer
from concourse.mybir import AluOpType, ActivationFunctionType

N, R, LIST, BAGS, SIM = 8, 8192, 2048, 256, 256
WHO = (0, 0, 0, 1, 1, 2, 2, 2)
ORDER = (5, 3, 1, 6, 2, 4, 7)
SEND = (1, 2, 5, 3, 6, 4, 7)
CUT = (1600, 1408, 1216)
PLACES = max(WHO) + 1
NL = max([WHO.count(_k) for _k in range(PLACES)])
BIG = 9.999e29
PAD = 8
WIN = R + 2 * PAD
MW = 2312
SW = 2056
LW = 160
SIZES = (2048, 2048, 2048, 2048)
HOME = (1, 2, 1, 2)
EARLY = 3
FIRST = 1
CH = len(SIZES)

SCRATCH = {
    "win": ("sbuf", [128, WIN], "bfloat16"),
    "ii": ("sbuf", [16, 128], "int32"),
    "en": ("sbuf", [16, 16], "int32"),
    "pv": ("sbuf", [16, 16], "int32"),
    "dd": ("sbuf", [16, 16], "float32"),
    "t1": ("sbuf", [16, 16], "float32"),
    "t2": ("sbuf", [16, 16], "float32"),
    "t3": ("sbuf", [16, 16], "float32"),
    "ie": ("sbuf", [16, 128], "float32"),
    "sele": ("sbuf", [16, 128], "float32"),
    "wl": ("sbuf", [16, NL * LW], "float32"),
    "wsend": ("dram", [128, 20], "float32"),
    "wland": ("dram", [NL, 128, 20], "float32"),
    "offs": ("sbuf", [128, NL * 160], "uint16"),
    "neg": ("sbuf", [128, 1024], "bfloat16"),
    "res": ("sbuf", [128, NL * BAGS], "bfloat16"),
    "rland": ("sbuf", [128, N * BAGS], "bfloat16"),
    "acc": ("sbuf", [128, BAGS], "bfloat16"),
    "pacc": ("psum", [128, 512], "float32"),
}
for _k in range(NL):
    SCRATCH["gat%d" % _k] = ("sbuf", [128, LIST], "bfloat16")
    SCRATCH["msk%d" % _k] = ("sbuf", [128, MW], "bfloat16")
    SCRATCH["scn%d" % _k] = ("sbuf", [128, SW], "bfloat16")
    SCRATCH["ps%d" % _k] = ("psum", [128, 512], "float32")
SEMAPHORES = ["pz", "on", "wf", "ng", "zs", "ldx", "dio", "sele_", "e1", "e2", "snd", "sto", "loc", "ac", "st"]
for _k in range(NL):
    SEMAPHORES += [_n + "%d" % _k for _n in ("mk", "pe", "wl", "of", "sc", "vg", "sg", "sn", "fi")]
for _k in range(CH):
    SEMAPHORES += ["ld%d" % _k, "tc%d" % _k]
for _k in range(N):
    SEMAPHORES += ["l%d" % _k, "r%d" % _k]


def team(c, topo):
    near = [d for d in range(SIM) if d != c and topo.host(d) == topo.host(c) and topo.chip(d) == topo.chip(c)
            and topo.die(d) == topo.die(c)]
    return ([c] + near)[:PLACES]


def bits(m):
    return bin(m).count("1")


def rank_program(g, core, T, topo):
    me = None
    for r, c in enumerate(T.cores):
        if topo.host(c) == topo.host(core) and topo.chip(c) == topo.chip(core):
            crew = team(c, topo)
            if core in crew:
                me = (r, crew.index(core))
    if me is None:
        return
    r, place = me
    V, S, P, Y = g.vector, g.scalar, g.tensor, g.sync
    A, F = AluOpType, ActivationFunctionType
    sem = T.sem
    js = [j for j in range(N) if WHO[j] == place]
    nl = len(js)
    last = nl - 1
    is_rank = place == 0

    def chunk(c):
        a = PAD + sum(SIZES[:c])
        return T.win[:, a:a + SIZES[c]]

    def came(c):
        return bits(topo.mask(crew[0 if HOME[c] == place else HOME[c]], core))

    def table(q):
        q.wait_ge(sem.wf, 2)
        for c in range(CH):
            q.wait_ge(sem["ld%d" % c] if is_rank else sem["tc%d" % c], 16 if is_rank else came(c))

    cut = [CUT[0] if is_rank else CUT[2]] * nl
    if is_rank:
        cut[last] = CUT[1]

    if is_rank:
        S.dma_start(out=T.ii[:, :], in_=T.idx[:, :]).then_inc(sem.ldx, 16)
        Y.dma_start(out=T.en[:, :], in_=T.end[:, :]).then_inc(sem.ldx, 16)
        S.wait_ge(sem.pz, 1)
        S.dma_start(out=T.pv[0:1, 1:16], in_=T.end[15:16, 0:15]).then_inc(sem.ldx, 16)
        Y.wait_ge(sem.pz, 1)
        Y.dma_start(out=T.pv[1:16, :], in_=T.end[0:15, :]).then_inc(sem.ldx, 16)
        for c in range(CH):
            if c == EARLY:
                Y.wait_ge(sem.snd, 2)
                Y.wait_ge(sem.e2, 2)
                Y.dma_start(out=T.wsend[:, :], in_=T.wl[:, 0:LW]).then_inc(sem.sto, 16)
            a = sum(SIZES[:c])
            Y.dma_start(out=chunk(c), in_=T.tab[:, a:a + SIZES[c]]).then_inc(sem["ld%d" % c], 16)
    for k in range(nl):
        if js[k]:
            src = (r + js[k]) % N
            Y.wait_ge(sem["l%d" % src], bits(topo.mask(T.cores[src], core)))
            Y.dma_start(out=T.wl[:, k * LW:(k + 1) * LW], in_=T.wland[k]).then_inc(sem["wl%d" % k], 16)

    if is_rank:
        V.memset(T.pv[:, :], 0).then_inc(sem.pz, 1)
    V.memset(T.neg[:, :], -BIG).then_inc(sem.ng, 1)
    V.wait_ge(sem.on, 1)
    V.tensor_scalar(T.sele[:, :], T.ie[:, :], 0.0, None, op0=A.is_equal).then_inc(sem.sele_, 1)
    V.memset(T.win[:, 0:PAD], -BIG).then_inc(sem.wf, 1)
    V.memset(T.win[:, PAD + R:WIN], -BIG).then_inc(sem.wf, 1)

    if is_rank:
        V.wait_ge(sem.ldx, 64)
        V.wait_ge(sem.dio, 1)
        V.tensor_tensor(T.t1[:, :], T.en[:, :], T.pv[:, :], A.is_gt).then_inc(sem.e1, 1)
        V.tensor_tensor(T.t2[:, :], T.en[:, :], T.pv[:, :], A.is_le).then_inc(sem.e1, 1)
        V.tensor_copy(T.wl[:, 0:128], T.ii[:, :]).then_inc(sem.snd, 1)
        V.wait_ge(sem.e1, 2)
        V.tensor_tensor(T.wl[:, 144:160], T.en[:, :], T.t1[:, :], A.mult).then_inc(sem.e2, 1)
        V.tensor_tensor(T.t3[:, :], T.dd[:, :], T.t2[:, :], A.mult).then_inc(sem.e2, 1)
        V.wait_ge(sem.e2, 2)
        V.tensor_tensor(T.wl[:, 128:144], T.wl[:, 144:160], T.t3[:, :], A.add).then_inc(sem.snd, 1)

    by_s = range(2, nl) if is_rank else ()
    mk = {}

    def base(k):
        V.memset(T["msk%d" % k][:, 0:1], -BIG).then_inc(sem["mk%d" % k], 1)
        if k in by_s:
            V.memset(T["msk%d" % k][:, 1:8], BIG).then_inc(sem["mk%d" % k], 1)
            V.memset(T["msk%d" % k][:, 2056:MW], BIG).then_inc(sem["mk%d" % k], 1)
            mk[k] = 5
        else:
            V.memset(T["msk%d" % k][:, 1:MW], BIG).then_inc(sem["mk%d" % k], 1)
            mk[k] = 2

    def offsets(k):
        V.wait_ge(sem["pe%d" % k], 1)
        V.tensor_scalar(T.offs[:, k * 160:k * 160 + 128], T["ps%d" % k][:, 0:128], float(PAD - R * r), float(PAD + R),
                        op0=A.add, op1=A.min).then_inc(sem["of%d" % k], 1)
        V.tensor_copy(T.offs[:, k * 160 + 128:(k + 1) * 160], T["ps%d" % k][:, 128:160]).then_inc(sem["of%d" % k], 1)

    def marks(k):
        V.wait_ge(sem["of%d" % k], 2)
        V.wait_ge(sem.ng, 1)
        V.wait_ge(sem["mk%d" % k], mk[k])
        V.tensor_copy(T["msk%d" % k][:, :].indirect(T.offs[:, k * 160 + 128:k * 160 + 144]), T.neg[:, 0:BAGS]).then_inc(sem["sc%d" % k], 1)

    def gather_v(k):
        V.wait_ge(sem["of%d" % k], 2)
        V.tensor_copy(T["gat%d" % k][:, cut[k]:LIST],
                      T.win[:, :].indirect(T.offs[:, k * 160 + cut[k] // 16:k * 160 + 128])).then_inc(sem["vg%d" % k], 1)

    def scan(k):
        V.wait_ge(sem["sc%d" % k], 1)
        V.wait_ge(sem["vg%d" % k], 1)
        V.wait_ge(sem["sg%d" % k], 1)
        V.tensor_tensor_scan(T["scn%d" % k][:, 2:2 + LIST], T["msk%d" % k][:, 0:LIST], T["gat%d" % k][:, :], 0.0,
                             A.min, A.max).then_inc(sem["sn%d" % k], 1)

    def target(k):
        return (T.rland, 0) if js[k] == 0 else (T.res, k * BAGS)

    half = BAGS // 2
    if is_rank:
        base(0)
        offsets(0)
        marks(0)
        for k in range(1, nl):
            base(k)
    else:
        for k in range(nl):
            base(k)
    for k in range(nl):
        V.memset(T["scn%d" % k][:, 0:2], 0.0).then_inc(sem.zs, 1)
    if is_rank:
        table(V)
        gather_v(0)
        scan(0)
        for k in range(1, nl):
            offsets(k)
            marks(k)
            gather_v(k)
            scan(k)
    else:
        for k in range(nl):
            offsets(k)
        for k in range(nl):
            marks(k)
        table(V)
        for k in range(nl):
            gather_v(k)
            scan(k)
    V.wait_ge(sem["sn%d" % last], 1)
    V.wait_ge(sem.zs, nl)
    buf, a = target(last)
    V.tensor_copy(buf[:, a + half:a + BAGS], T["scn%d" % last][:, 1:2 + LIST].indirect(T.offs[:, last * 160 + 152:last * 160 + 160])).then_inc(sem["fi%d" % last], 1)
    if is_rank:
        V.wait_ge(sem.fi0, 1)
        for n_, j in enumerate(ORDER):
            frm = team(T.cores[(r - j) % N], topo)[WHO[j]]
            V.wait_ge(sem["r%d" % j], bits(topo.mask(frm, core)))
            if n_:
                V.wait_ge(sem.ac, n_)
            V.tensor_tensor(T.acc[:, :] if n_ == len(ORDER) - 1 else T.pacc[:, 0:BAGS],
                            T.pacc[:, 0:BAGS] if n_ else T.rland[:, 0:BAGS],
                            T.rland[:, j * BAGS:(j + 1) * BAGS], A.max).then_inc(sem.ac, 1)
        Y.wait_ge(sem.ac, len(ORDER))
        Y.dma_start(out=T.y[:, :], in_=T.acc[:, :]).then_inc(sem.st, 16)
        Y.wait_ge(sem.st, 16)

    P.wait_ge(sem.sele_, 1)
    for k in range(nl):
        if js[k] == 0:
            P.wait_ge(sem.snd, 2)
            P.wait_ge(sem.e2, 2)
        else:
            P.wait_ge(sem["wl%d" % k], 16)
        P.matmul(T["ps%d" % k][:, 0:LW], T.sele[:, :], T.wl[:, k * LW:(k + 1) * LW], True, True).then_inc(sem["pe%d" % k], 1)

    if by_s:
        S.wait_ge(sem.ng, 1)
    for k in by_s:
        for a in (8, 1032):
            S.activation(T["msk%d" % k][:, a:a + 1024], T.neg[:, :], F.Copy, scale=-1.0).then_inc(sem["mk%d" % k], 1)

    def fetch(k, n):
        S.wait_ge(sem["sn%d" % k], 1)
        S.wait_ge(sem.zs, nl)
        buf, a = target(k)
        S.activation(buf[:, a:a + n], T["scn%d" % k][:, 1:2 + LIST].indirect(T.offs[:, k * 160 + 144:k * 160 + 144 + n // 16]), F.Copy).then_inc(sem["fi%d" % k], 1)

    for k in range(nl):
        S.wait_ge(sem["of%d" % k], 2)
        if k == 0:
            table(S)
        S.activation(T["gat%d" % k][:, 0:cut[k]], T.win[:, :].indirect(T.offs[:, k * 160:k * 160 + cut[k] // 16]),
                     F.Copy).then_inc(sem["sg%d" % k], 1)
        if k:
            fetch(k - 1, BAGS)
    fetch(last, half)

    sent = 0
    g.iota(T.ie[:, :], [[0, 8], [-1, 16]], 0, 1, allow_small_or_imprecise_dtypes=True).then_inc(sem.on, 1)
    if is_rank:
        g.iota(T.dd[:, :], [[16, 16]], LIST + 1, 1, allow_small_or_imprecise_dtypes=True).then_inc(sem.dio, 1)
    for c in range(CH):
        if is_rank and c == FIRST:
            ids, dsts, m = [], [], None
            for j in SEND:
                d = team(T.cores[(r - j) % N], topo)[WHO[j]]
                slot = [q for q in range(N) if WHO[q] == WHO[j]].index(j)
                rid, pid = topo.addr(d, core)
                ids.append(DstId(rid=rid, pnc=pid))
                dsts.append(T.wland[slot])
                m = topo.mask(core, d)
            g.wait_ge(sem.sto, 16)
            g.remote_dma_fused([RemoteDMATransfer(dst_ids=ids, dma_engine_mask=m, remote_sem=sem["l%d" % r],
                                                  srcs=[T.wsend[:, :]], dsts=dsts)], local_sem=sem.loc)
            sent += bits(m)
        if not is_rank and HOME[c] != place:
            continue
        g.wait_ge(sem["ld%d" % c] if is_rank else sem["tc%d" % c], 16 if is_rank else came(c))
        for p in [HOME[c]] if is_rank else [p for p in range(1, PLACES) if p != place]:
            m = topo.mask(core, crew[p])
            rid, pid = topo.addr(crew[p], core)
            g.remote_dma(chunk(c), chunk(c), sem["tc%d" % c], sem.loc, pid, rid, m)
            sent += bits(m)
    for k in range(nl):
        if js[k] == 0:
            continue
        d = T.cores[(r + js[k]) % N]
        m = topo.mask(core, d)
        rid, pid = topo.addr(d, core)
        g.wait_ge(sem["fi%d" % k], 2 if k == last else 1)
        g.remote_dma(T.rland[:, js[k] * BAGS:(js[k] + 1) * BAGS], T.res[:, k * BAGS:(k + 1) * BAGS], sem["r%d" % js[k]], sem.loc,
                     pid, rid, m)
        sent += bits(m)
    g.wait_ge(sem.loc, sent)
